import numpy as np
import ml_dtypes


def mxq(x, axis, fmt="e4m3"):
    dtype, down = {"e4m3": (ml_dtypes.float8_e4m3fn, 7), "e5m2": (ml_dtypes.float8_e5m2, 14)}[fmt]
    v = np.moveaxis(np.asarray(x, np.float32).astype(ml_dtypes.bfloat16).astype(np.float64), axis, -1)
    blocks = v.reshape(v.shape[:-1] + (-1, 32))
    amax = np.abs(blocks).max(-1, keepdims=True)
    byte = np.maximum(np.where(amax > 0, np.frexp(amax)[1] - 1 + 127, 0) - down, 1)
    scale = np.exp2(byte - 127.0)
    codes = (blocks / scale).astype(np.float32).astype(dtype).astype(np.float64)
    return np.moveaxis((codes * scale).reshape(v.shape), -1, axis)


WIDE = False


def mx_kscale(k):
    if not WIDE:
        return np.ones(k)
    levels = np.array([10, -10, 5, -5, 0])
    if k % 512:
        return np.exp2(np.random.permutation(np.resize(levels, k // 32))).repeat(32)
    a = np.empty((k // 512, 16))
    for p in range(k // 512):
        a[p, :8] = np.random.permutation(np.resize(levels, 8))
        for g in range(8):
            far = levels[np.abs(levels - a[p, g]) >= 10]
            a[p, g + 8] = far[np.random.randint(len(far))]
    return np.exp2(a.ravel()).repeat(32)


def f64(x):
    return np.asarray(x).astype(np.float64)


def striped(idx):
    return np.tile(idx.reshape(-1, 16).T, (8, 1)).astype(np.uint16)


def unstriped(offs):
    return offs[:16].T.reshape(-1).astype(np.int64)


def striped8(idx):
    return np.concatenate([x.reshape(-1, 16).T for x in idx]).astype(np.uint16)


def runs(offs, k):
    lists = np.stack([offs[16 * r : 16 * r + 16].T.reshape(-1) for r in range(8)]).astype(np.int64)
    return lists[np.arange(k) % 512 // 64]


def pack_weight(w):
    k, n = w.shape
    w = f64(np.asarray(w, np.float32).astype(ml_dtypes.bfloat16)).reshape(k // 32, 32, n)
    amax = np.abs(w).max(1)
    byte = np.clip(np.where(amax > 0, np.frexp(amax)[1] - 1 + 127 - 7, 1), 1, 254)
    scaled = (w * np.exp2(127.0 - byte)[:, None, :]).reshape(k, n).astype(np.float32)
    words = np.ascontiguousarray(scaled.reshape(k // 512, 128, 4, n).transpose(0, 1, 3, 2)).astype(ml_dtypes.float8_e4m3fn).view(np.uint8)
    return words, np.ascontiguousarray(byte.astype(np.uint8).reshape(k // 512, 16, n))


def unpack_weight(words, scales):
    g, p, n, _ = words.shape
    vals = np.ascontiguousarray(words).view(ml_dtypes.float8_e4m3fn).astype(np.float64) * np.repeat(np.exp2(scales.astype(np.float64) - 127.0), 8, axis=1)[..., None]
    return vals.transpose(0, 1, 3, 2).reshape(g * 512, n)


def relu(v):
    return np.maximum(v, 0.0)


K, T, S, N, H = 512, 2048, 512, 512, 512


def setup_inputs():
    n = np.random.standard_normal
    s = mx_kscale(K)[:, None]
    u = mx_kscale(H)
    packed_xT = pack_weight(n((K, T)) * s)
    return {
        "x_words": packed_xT[0],
        "x_scales": packed_xT[1],
        "w1": (n((K, H)) / np.sqrt(K) / s * u).astype(np.float32),
        "w2": (n((H, H)) / np.sqrt(H) / u[:, None] * u).astype(np.float32),
        "res": (2 * n((N, S))).astype(np.float32),
        "w3": (n((H, N)) / np.sqrt(H) / u[:, None]).astype(np.float32),
        "offs": striped(np.random.permutation(T)[:S]),
        "s1": striped8(np.stack([np.random.permutation(S) for _ in range(8)])),
        "s2": striped8(np.stack([np.random.permutation(S) for _ in range(8)])),
    }


def reference(x_words, x_scales, w1, w2, res, w3, offs, s1, s2):
    xq = unpack_weight(x_words, x_scales)[:, unstriped(offs)]
    y = relu(mxq(f64(w1), 0, "e4m3").T @ xq)
    z = y[np.arange(H)[:, None], runs(s1, H)]
    h = relu(mxq(f64(w2), 0, "e4m3").T @ mxq(z, 0, "e4m3"))
    z2 = h[np.arange(H)[:, None], runs(s2, H)]
    return f64(res) + (mxq(f64(w3), 0, "e4m3").T @ mxq(z2, 0, "e4m3"))

@@ -1,0 +1,187 @@
+from contextlib import ExitStack
+
+import concourse.mybir as mybir
+
+K, T, S, N, H = 512, 2048, 512, 512, 512
+FLOPS = 2 * S * (K * H + H * H + H * N)
+
+F32 = mybir.dt.float32
+BF16 = mybir.dt.bfloat16
+I32 = mybir.dt.int32
+U32 = mybir.dt.uint32
+U16 = mybir.dt.uint16
+U8 = mybir.dt.uint8
+FP8X4 = mybir.dt.float8_e4m3fn_x4
+RELU = mybir.ActivationFunctionType.Relu
+COPY = mybir.ActivationFunctionType.Copy
+ADD = mybir.AluOpType.add
+
+P = 128
+PACK = 4
+LANES = 16
+W2_SPLIT = 256
+PIECES = ((0, 256), (256, 128), (384, 128))
+
+
+def tile_picked_shuf3_relu_p_kernel(
+    tc, x_words, x_scales, w1, w2, res, w3, offs, s1, s2, out
+):
+    nc = tc.nc
+    with ExitStack() as ctx:
+        lists = ctx.enter_context(tc.tile_pool(name="lists", bufs=1))
+        sb = ctx.enter_context(tc.tile_pool(name="sb", bufs=1))
+        psum = ctx.enter_context(tc.psum_pool(name="psum", bufs=1))
+
+        def entries(list_tile, first, count):
+            return list_tile[:, first // LANES : (first + count) // LANES]
+
+        def mx(acc, codes_l, scales_l, codes_r, scales_r):
+            nc.tensor.matmul_mx(
+                out=acc,
+                lhsT=codes_l.bitcast(FP8X4),
+                lhsT_scale=scales_l,
+                rhs=codes_r.bitcast(FP8X4),
+                rhs_scale=scales_r,
+                start=True,
+                stop=True,
+            )
+
+        def quantize(codes, scales, grouped):
+            nc.vector.quantize_mx(out=codes.bitcast(FP8X4), scales=scales, in_=grouped)
+
+        offs_t = lists.tile([P, S // LANES], U16, name="offs_t")
+        s1_t = lists.tile([P, S // LANES], U16, name="s1_t")
+        s2_t = lists.tile([P, S // LANES], U16, name="s2_t")
+        xw = sb.tile([P, T], U32, name="xw", align_bytes=64)
+        xs = sb.tile([P, T], U8, name="xs", align_bytes=64)
+        w1_raw = sb.tile([P, PACK, H], F32, name="w1_raw")
+        w2_raw = [sb.tile([P, PACK, n], F32, name="w2_raw%d" % a) for a, n in enumerate((W2_SPLIT, H - W2_SPLIT))]
+        w3_raw = sb.tile([P, PACK, N], F32, name="w3_raw")
+        res_t = sb.tile([P, N // P, S], F32, name="res_t")
+
+        nc.vector.memset(xs[:].bitcast(I32), 0)
+        warm = sb.tile([P, 2], F32, name="warm")
+        nc.gpsimd.memset(warm[:, 0:1], 0.0)
+        nc.scalar.activation(warm[:, 1:2], warm[:, 0:1], RELU)
+        w1_rows = w1.rearrange("(p j) n -> p j n", j=PACK)
+        nc.sync.dma_start(w1_raw[:, 0, :], w1_rows[:, 0, :])
+        nc.sync.dma_start(offs_t[:], offs)
+        nc.sync.dma_start(s1_t[:], s1)
+        nc.sync.dma_start(s2_t[:], s2)
+        for j in range(1, PACK):
+            nc.sync.dma_start(w1_raw[:, j, :], w1_rows[:, j, :])
+        for q in range(4):
+            nc.sync.dma_start(
+                xs[32 * q : 32 * q + 4, :].bitcast(I32), x_scales[0, 4 * q : 4 * q + 4, :].bitcast(I32)
+            )
+        nc.sync.dma_start(xw[:].bitcast(I32), x_words[0].rearrange("p n t -> p (n t)").bitcast(I32))
+        w2_rows = w2.rearrange("(p j) n -> p j n", j=PACK)
+        nc.sync.dma_start(w2_raw[0][:], w2_rows[:, :, 0:W2_SPLIT])
+        nc.sync.dma_start(w2_raw[1][:], w2_rows[:, :, W2_SPLIT:H])
+        nc.sync.dma_start(w3_raw[:], w3.rearrange("(p j) n -> p j n", j=PACK))
+        nc.sync.dma_start(res_t[:], res.rearrange("(b p) j -> p b j", p=P))
+
+        w1_codes = sb.tile([P, H], U32, name="w1_codes", align_bytes=64)
+        w1_scales = sb.tile([P, H], U8, name="w1_scales", align_bytes=64)
+        w1_dealt = w1_raw[:].rearrange("p j (m t) -> p m j t", t=PACK)
+        w1_g = [sb.tile([P, 2, P, PACK], BF16, name="w1_g%d" % a, align_bytes=64) for a in range(2)]
+        nc.vector.tensor_copy(w1_g[0][:].rearrange("p t m j -> p m j t"), w1_dealt[:, :, :, 0:2])
+        nc.scalar.copy(w1_g[1][:].rearrange("p t m j -> p m j t"), w1_dealt[:, :, :, 2:4])
+        xg_s = sb.tile([P, S], U8, name="xg_s", align_bytes=64)
+        nc.vector.tensor_copy(xg_s[:], xs[:].indirect(offs_t[:]))
+        for a in range(2):
+            cols = slice(a * 256, (a + 1) * 256)
+            quantize(w1_codes[:, cols], w1_scales[:, cols], w1_g[a][:].rearrange("p t m j -> p (t m j)"))
+        xg_w = sb.tile([P, S], U32, name="xg_w", align_bytes=64)
+        for a in range(2):
+            nc.vector.tensor_copy(xg_w[:, a * 256 : (a + 1) * 256], xw[:].indirect(entries(offs_t, a * 256, 256)))
+
+        y = [sb.tile([P, S], F32, name="y%d" % t) for t in range(PACK)]
+        for t in range(PACK):
+            rows = slice(t * P, (t + 1) * P)
+            for a in range(2):
+                cols = slice(a * 256, (a + 1) * 256)
+                y_acc = psum.tile([P, 256], F32, name="y_acc%d%d" % (t, a), tag="bank%d" % (PACK * a + t))
+                mx(y_acc[:], w1_codes[:, rows], w1_scales[:, rows], xg_w[:, cols], xg_s[:, cols])
+                nc.scalar.activation(y[t][:, cols], y_acc[:], RELU)
+
+        w2_g = sb.tile([P, PACK, P, PACK], BF16, name="w2_g", align_bytes=64)
+        w2_out = w2_g[:].rearrange("p (u t) m j -> p u m j t", u=2)
+        deal = "p j (m u t) -> p u m j t"
+        nc.vector.tensor_copy(w2_out[:, :, 0 : W2_SPLIT // PACK], w2_raw[0][:].rearrange(deal, u=2, t=2))
+        nc.scalar.copy(w2_out[:, :, W2_SPLIT // PACK : P], w2_raw[1][:].rearrange(deal, u=2, t=2))
+        w2_codes = sb.tile([P, H], U32, name="w2_codes", align_bytes=64)
+        w2_scales = sb.tile([P, H], U8, name="w2_scales", align_bytes=64)
+
+        def shuffle(rows_f32, list_tile, label, before_quantize, early):
+            def gather(q, tag):
+                first, count = PIECES[q]
+                plane = sb.tile([P, PACK, count], BF16, name="%s_p%d" % (label, q), tag=tag, align_bytes=64)
+                for t in range(PACK):
+                    nc.vector.tensor_copy(plane[:, t, :], rows_f32[t][:].indirect(entries(list_tile, first, count)))
+                return plane
+
+            def weave(q, plane):
+                count = PIECES[q][1]
+                w = sb.tile([P, count * PACK], BF16, name="%s_w%d" % (label, q), align_bytes=64)
+                nc.scalar.copy(
+                    w[:].rearrange("p (c i t) -> p c t i", i=4, t=PACK),
+                    plane[:].rearrange("p t (c i) -> p c t i", i=4),
+                )
+                return w
+
+            def pack(q, w):
+                count = PIECES[q][1]
+                codes = sb.tile([P, count], U32, name="%s_c%d" % (label, q), align_bytes=64)
+                scales = sb.tile([P, count], U8, name="%s_s%d" % (label, q), align_bytes=64)
+                quantize(codes[:], scales[:], w[:])
+                return codes, scales
+
+            woven = [weave(q, gather(q, "%s_p%d" % (label, q))) for q in range(3)]
+            if early:
+                before_quantize()
+                return [pack(q, woven[q]) for q in range(3)]
+            made = [pack(0, woven[0])]
+            before_quantize()
+            return made + [pack(q, woven[q]) for q in (1, 2)]
+
+        z = shuffle(y, s1_t, "z", lambda: quantize(w2_codes[:], w2_scales[:], w2_g[:].rearrange("p t m j -> p (t m j)")), True)
+
+        h = [sb.tile([P, S], F32, name="h%d" % t, align_bytes=64) for t in range(PACK)]
+        for t in range(PACK):
+            rows = slice(t * P, (t + 1) * P)
+            for a in range(2):
+                h_acc = psum.tile([P, 256], F32, name="h_acc%d%d" % (t, a), tag="bank%d" % (PACK * a + t))
+                for (first, count), (codes, scales) in zip(PIECES, z):
+                    if first // 256 == a:
+                        mx(h_acc[:, first % 256 : first % 256 + count], w2_codes[:, rows], w2_scales[:, rows], codes[:], scales[:])
+                nc.scalar.activation(h[t][:, a * 256 : (a + 1) * 256], h_acc[:], RELU)
+
+        w3_src = w3_raw[:].rearrange("p j (c i) -> p c j i", i=4)
+        w3_g0 = sb.tile([P, 256 * PACK], BF16, name="w3_g0", align_bytes=64, tag="z_p2")
+        w3_g1 = sb.tile([P, 256 * PACK], BF16, name="w3_g1", align_bytes=64, tag="z_w2")
+        nc.scalar.copy(w3_g0[:].rearrange("p (c i j) -> p c j i", i=4, j=PACK), w3_src[:, 0:64])
+        nc.vector.tensor_copy(w3_g1[:].rearrange("p (c i j) -> p c j i", i=4, j=PACK), w3_src[:, 64:128])
+        w3_codes = [sb.tile([P, 256], U32, name="w3_codes0", align_bytes=64)]
+        w3_scales = [sb.tile([P, 256], U8, name="w3_scales%d" % a, align_bytes=64) for a in range(2)]
+        quantize(w3_codes[0][:], w3_scales[0][:], w3_g0[:])
+
+        def late_half():
+            w3_codes.append(sb.tile([P, 256], U32, name="w3_codes1", align_bytes=64, tag="h3"))
+            quantize(w3_codes[1][:], w3_scales[1][:], w3_g1[:])
+
+        z2 = shuffle(h, s2_t, "zz", late_half, False)
+
+        out_rows = out.rearrange("(b p) j -> p b j", p=P)
+        bank = 0
+        for (first, count), (codes, scales) in zip(PIECES, z2):
+            per_bank = S // count
+            for b0 in range(0, N // P, per_bank):
+                acc = psum.tile([P, per_bank, count], F32, name="o_acc%d" % bank, tag="bank%d" % bank)
+                for b in range(per_bank):
+                    half, rows = (b0 + b) // 2, slice((b0 + b) % 2 * P, ((b0 + b) % 2 + 1) * P)
+                    mx(acc[:, b, :], w3_codes[half][:, rows], w3_scales[half][:, rows], codes[:], scales[:])
+                o = sb.tile([P, per_bank, count], F32, name="o%d" % bank)
+                nc.vector.tensor_tensor(o[:], acc[:], res_t[:, b0 : b0 + per_bank, first : first + count], ADD)
+                nc.sync.dma_start(out_rows[:, b0 : b0 + per_bank, first : first + count], o[:])
+                bank = bank + 1

@@ -55,8 +55,10 @@ def tile_picked_shuf3_relu_p_kernel(
         xw = sb.tile([P, T], U32, name="xw", align_bytes=64)
         xs = sb.tile([P, T], U8, name="xs", align_bytes=64)
         w1_raw = sb.tile([P, PACK, H], F32, name="w1_raw")
-        w2_raw = [sb.tile([P, PACK, n], F32, name="w2_raw%d" % a) for a, n in enumerate((W2_SPLIT, H - W2_SPLIT))]
-        w3_raw = sb.tile([P, PACK, N], F32, name="w3_raw")
+        w2_lo = sb.tile([P, PACK, 256], F32, name="w2_lo", align_bytes=64)
+        reused = sb.tile([P, 512 + 1024], F32, name="reused", align_bytes=64)
+        w2_raw = [w2_lo[:], reused[:, 512:1536].rearrange("p (j n) -> p j n", j=PACK)]
+        w3_raw = sb.tile([P, PACK, N], F32, name="w3_raw", align_bytes=64)
         res_t = sb.tile([P, N // P, S], F32, name="res_t")
 
         nc.vector.memset(xs[:].bitcast(I32), 0)
@@ -64,10 +66,10 @@ def tile_picked_shuf3_relu_p_kernel(
         nc.gpsimd.memset(warm[:, 0:1], 0.0)
         nc.scalar.activation(warm[:, 1:2], warm[:, 0:1], RELU)
         w1_rows = w1.rearrange("(p j) n -> p j n", j=PACK)
-        nc.sync.dma_start(w1_raw[:, 0, :], w1_rows[:, 0, :])
+        nc.sync.dma_start(w1_raw[:, 0, 0:256], w1_rows[:, 0, 0:256])
         nc.sync.dma_start(offs_t[:], offs)
         nc.sync.dma_start(s1_t[:], s1)
-        nc.sync.dma_start(s2_t[:], s2)
+        nc.sync.dma_start(w1_raw[:, 0, 256:512], w1_rows[:, 0, 256:512])
         for j in range(1, PACK):
             nc.sync.dma_start(w1_raw[:, j, :], w1_rows[:, j, :])
         for q in range(4):
@@ -76,17 +78,19 @@ def tile_picked_shuf3_relu_p_kernel(
             )
         nc.sync.dma_start(xw[:].bitcast(I32), x_words[0].rearrange("p n t -> p (n t)").bitcast(I32))
         w2_rows = w2.rearrange("(p j) n -> p j n", j=PACK)
-        nc.sync.dma_start(w2_raw[0][:], w2_rows[:, :, 0:W2_SPLIT])
-        nc.sync.dma_start(w2_raw[1][:], w2_rows[:, :, W2_SPLIT:H])
+        nc.sync.dma_start(w2_raw[0], w2_rows[:, :, 0:W2_SPLIT])
+        nc.sync.dma_start(w2_raw[1], w2_rows[:, :, W2_SPLIT:H])
         nc.sync.dma_start(w3_raw[:], w3.rearrange("(p j) n -> p j n", j=PACK))
+        nc.sync.dma_start(s2_t[:], s2)
         nc.sync.dma_start(res_t[:], res.rearrange("(b p) j -> p b j", p=P))
 
         w1_codes = sb.tile([P, H], U32, name="w1_codes", align_bytes=64)
         w1_scales = sb.tile([P, H], U8, name="w1_scales", align_bytes=64)
         w1_dealt = w1_raw[:].rearrange("p j (m t) -> p m j t", t=PACK)
         w1_g = [sb.tile([P, 2, P, PACK], BF16, name="w1_g%d" % a, align_bytes=64) for a in range(2)]
-        nc.vector.tensor_copy(w1_g[0][:].rearrange("p t m j -> p m j t"), w1_dealt[:, :, :, 0:2])
-        nc.scalar.copy(w1_g[1][:].rearrange("p t m j -> p m j t"), w1_dealt[:, :, :, 2:4])
+        w1_out = [g[:].rearrange("p t m j -> p m j t") for g in w1_g]
+        nc.vector.tensor_copy(w1_out[0], w1_dealt[:, :, :, 0:2])
+        nc.scalar.copy(w1_out[1], w1_dealt[:, :, :, 2:4])
         xg_s = sb.tile([P, S], U8, name="xg_s", align_bytes=64)
         nc.vector.tensor_copy(xg_s[:], xs[:].indirect(offs_t[:]))
         for a in range(2):
@@ -96,88 +100,92 @@ def tile_picked_shuf3_relu_p_kernel(
         for a in range(2):
             nc.vector.tensor_copy(xg_w[:, a * 256 : (a + 1) * 256], xw[:].indirect(entries(offs_t, a * 256, 256)))
 
-        y = [sb.tile([P, S], F32, name="y%d" % t) for t in range(PACK)]
-        for t in range(PACK):
-            rows = slice(t * P, (t + 1) * P)
-            for a in range(2):
-                cols = slice(a * 256, (a + 1) * 256)
-                y_acc = psum.tile([P, 256], F32, name="y_acc%d%d" % (t, a), tag="bank%d" % (PACK * a + t))
-                mx(y_acc[:], w1_codes[:, rows], w1_scales[:, rows], xg_w[:, cols], xg_s[:, cols])
-                nc.scalar.activation(y[t][:, cols], y_acc[:], RELU)
+        def hidden_layer(label, codes_w, scales_w, codes, scales, first_bank):
+            result = [sb.tile([P, S], F32, name="%s%d" % (label, t), align_bytes=64) for t in range(PACK)]
+            bank = first_bank
+            for t in range(PACK):
+                rows = slice(t * P, (t + 1) * P)
+                width = 256 if t == 0 else S
+                for start in range(0, S, width):
+                    cols = slice(start, start + width)
+                    acc = psum.tile([P, width], F32, name="%s_acc%d" % (label, bank), tag="bank%d" % (bank % 8))
+                    mx(acc[:], codes_w[:, rows], scales_w[:, rows], codes[:, cols], scales[:, cols])
+                    nc.scalar.activation(result[t][:, cols], acc[:], RELU)
+                    bank = bank + 1
+            return result
+
+        y = hidden_layer("y", w1_codes, w1_scales, xg_w, xg_s, 0)
 
         w2_g = sb.tile([P, PACK, P, PACK], BF16, name="w2_g", align_bytes=64)
         w2_out = w2_g[:].rearrange("p (u t) m j -> p u m j t", u=2)
         deal = "p j (m u t) -> p u m j t"
-        nc.vector.tensor_copy(w2_out[:, :, 0 : W2_SPLIT // PACK], w2_raw[0][:].rearrange(deal, u=2, t=2))
-        nc.scalar.copy(w2_out[:, :, W2_SPLIT // PACK : P], w2_raw[1][:].rearrange(deal, u=2, t=2))
+        nc.vector.tensor_copy(w2_out[:, :, 0 : W2_SPLIT // PACK], w2_raw[0].rearrange(deal, u=2, t=2))
+        nc.scalar.copy(w2_out[:, :, W2_SPLIT // PACK : P], w2_raw[1].rearrange(deal, u=2, t=2))
         w2_codes = sb.tile([P, H], U32, name="w2_codes", align_bytes=64)
         w2_scales = sb.tile([P, H], U8, name="w2_scales", align_bytes=64)
 
-        def shuffle(rows_f32, list_tile, label, before_quantize, early):
-            def gather(q, tag):
-                first, count = PIECES[q]
-                plane = sb.tile([P, PACK, count], BF16, name="%s_p%d" % (label, q), tag=tag, align_bytes=64)
-                for t in range(PACK):
-                    nc.vector.tensor_copy(plane[:, t, :], rows_f32[t][:].indirect(entries(list_tile, first, count)))
-                return plane
-
-            def weave(q, plane):
-                count = PIECES[q][1]
-                w = sb.tile([P, count * PACK], BF16, name="%s_w%d" % (label, q), align_bytes=64)
-                nc.scalar.copy(
-                    w[:].rearrange("p (c i t) -> p c t i", i=4, t=PACK),
-                    plane[:].rearrange("p t (c i) -> p c t i", i=4),
+        def gather(plane, rows_f32, list_tile, piece):
+            first, count = piece
+            for t in range(PACK):
+                nc.vector.tensor_copy(
+                    plane[:, t * count : (t + 1) * count], rows_f32[t][:].indirect(entries(list_tile, first, count))
                 )
-                return w
 
-            def pack(q, w):
-                count = PIECES[q][1]
-                codes = sb.tile([P, count], U32, name="%s_c%d" % (label, q), align_bytes=64)
-                scales = sb.tile([P, count], U8, name="%s_s%d" % (label, q), align_bytes=64)
-                quantize(codes[:], scales[:], w[:])
-                return codes, scales
+        def weave(woven, plane):
+            nc.scalar.copy(
+                woven.rearrange("p (c i t) -> p c t i", i=4, t=PACK),
+                plane.rearrange("p (t c i) -> p c t i", i=4, t=PACK),
+            )
 
-            woven = [weave(q, gather(q, "%s_p%d" % (label, q))) for q in range(3)]
-            if early:
-                before_quantize()
-                return [pack(q, woven[q]) for q in range(3)]
-            made = [pack(0, woven[0])]
-            before_quantize()
-            return made + [pack(q, woven[q]) for q in (1, 2)]
+        def pack(label, q, woven, tag):
+            count = PIECES[q][1]
+            codes = sb.tile([P, count], U32, name="%s_c%d" % (label, q), align_bytes=64, tag=tag)
+            scales = sb.tile([P, count], U8, name="%s_s%d" % (label, q), align_bytes=64)
+            quantize(codes[:], scales[:], woven)
+            return codes, scales
 
-        z = shuffle(y, s1_t, "z", lambda: quantize(w2_codes[:], w2_scales[:], w2_g[:].rearrange("p t m j -> p (t m j)")), True)
+        def stage(name, q, dtype, tag=""):
+            return sb.tile([P, PACK * PIECES[q][1]], dtype, name=name, align_bytes=64, tag=tag or name)[:]
 
-        h = [sb.tile([P, S], F32, name="h%d" % t, align_bytes=64) for t in range(PACK)]
-        for t in range(PACK):
-            rows = slice(t * P, (t + 1) * P)
-            for a in range(2):
-                h_acc = psum.tile([P, 256], F32, name="h_acc%d%d" % (t, a), tag="bank%d" % (PACK * a + t))
-                for (first, count), (codes, scales) in zip(PIECES, z):
-                    if first // 256 == a:
-                        mx(h_acc[:, first % 256 : first % 256 + count], w2_codes[:, rows], w2_scales[:, rows], codes[:], scales[:])
-                nc.scalar.activation(h[t][:, a * 256 : (a + 1) * 256], h_acc[:], RELU)
+        z_woven = [sb.tile([P, 1024], BF16, name="z_w%d" % a, align_bytes=64) for a in range(2)]
+        z_plane = [stage("z_p0", 0, F32), reused[:, 0:1024]]
+        for a in range(2):
+            gather(z_plane[a], y, s1_t, (256 * a, 256))
+            weave(z_woven[a][:], z_plane[a])
+        quantize(w2_codes[:], w2_scales[:], w2_g[:].rearrange("p t m j -> p (t m j)"))
+        z_codes = sb.tile([P, S], U32, name="z_codes", align_bytes=64)
+        z_scales = sb.tile([P, S], U8, name="z_scales", align_bytes=64)
+        for a in range(2):
+            quantize(z_codes[:, 256 * a : 256 * (a + 1)], z_scales[:, 256 * a : 256 * (a + 1)], z_woven[a][:])
+
+        h = hidden_layer("h", w2_codes, w2_scales, z_codes, z_scales, 5)
 
         w3_src = w3_raw[:].rearrange("p j (c i) -> p c j i", i=4)
-        w3_g0 = sb.tile([P, 256 * PACK], BF16, name="w3_g0", align_bytes=64, tag="z_p2")
-        w3_g1 = sb.tile([P, 256 * PACK], BF16, name="w3_g1", align_bytes=64, tag="z_w2")
-        nc.scalar.copy(w3_g0[:].rearrange("p (c i j) -> p c j i", i=4, j=PACK), w3_src[:, 0:64])
-        nc.vector.tensor_copy(w3_g1[:].rearrange("p (c i j) -> p c j i", i=4, j=PACK), w3_src[:, 64:128])
-        w3_codes = [sb.tile([P, 256], U32, name="w3_codes0", align_bytes=64)]
+        w3_codes = [sb.tile([P, 256], U32, name="w3_codes%d" % a, align_bytes=64) for a in range(2)]
         w3_scales = [sb.tile([P, 256], U8, name="w3_scales%d" % a, align_bytes=64) for a in range(2)]
-        quantize(w3_codes[0][:], w3_scales[0][:], w3_g0[:])
+        for a, tag in enumerate(("reused", "z_scales")):
+            w3_g = sb.tile([P, 256 * PACK], BF16, name="w3_g%d" % a, align_bytes=64, tag=tag)
+            nc.scalar.copy(w3_g[:].rearrange("p (c i j) -> p c j i", i=4, j=PACK), w3_src[:, 64 * a : 64 * (a + 1)])
+            quantize(w3_codes[a][:], w3_scales[a][:], w3_g[:])
 
-        def late_half():
-            w3_codes.append(sb.tile([P, 256], U32, name="w3_codes1", align_bytes=64, tag="h3"))
-            quantize(w3_codes[1][:], w3_scales[1][:], w3_g1[:])
-
-        z2 = shuffle(h, s2_t, "zz", late_half, False)
+        shared = sb.tile([P, 256 + 512], F32, name="shared", align_bytes=64, tag="w3_raw")
+        zz_woven = [shared[:, 256:768].bitcast(BF16), stage("zz_w1", 1, BF16), stage("zz_w2", 2, BF16)]
+        zz_plane = [stage("zz_p0", 0, F32), stage("zz_p1", 1, F32), shared[:, 0:512]]
+        for q in range(2):
+            gather(zz_plane[q], h, s2_t, PIECES[q])
+            weave(zz_woven[q], zz_plane[q])
+        z2 = [pack("zz", 0, zz_woven[0], "zz_c0")]
+        gather(zz_plane[2], h, s2_t, PIECES[2])
+        weave(zz_woven[2], zz_plane[2])
+        z2.append(pack("zz", 1, zz_woven[1], "h3"))
+        z2.append(pack("zz", 2, zz_woven[2], "zz_c2"))
 
         out_rows = out.rearrange("(b p) j -> p b j", p=P)
         bank = 0
         for (first, count), (codes, scales) in zip(PIECES, z2):
-            per_bank = S // count
+            per_bank = 2 if first + count == S else S // count
             for b0 in range(0, N // P, per_bank):
-                acc = psum.tile([P, per_bank, count], F32, name="o_acc%d" % bank, tag="bank%d" % bank)
+                acc = psum.tile([P, per_bank, count], F32, name="o_acc%d" % bank, tag="bank%d" % ((bank + 2) % 8))
                 for b in range(per_bank):
                     half, rows = (b0 + b) // 2, slice((b0 + b) % 2 * P, ((b0 + b) % 2 + 1) * P)
                     mx(acc[:, b, :], w3_codes[half][:, rows], w3_scales[half][:, rows], codes[:], scales[:])

from contextlib import ExitStack

import concourse.mybir as mybir

K, T, S, N, H = 512, 2048, 512, 512, 512
FLOPS = 2 * S * (K * H + H * H + H * N)

F32 = mybir.dt.float32
BF16 = mybir.dt.bfloat16
I32 = mybir.dt.int32
U32 = mybir.dt.uint32
U16 = mybir.dt.uint16
U8 = mybir.dt.uint8
FP8X4 = mybir.dt.float8_e4m3fn_x4
RELU = mybir.ActivationFunctionType.Relu
COPY = mybir.ActivationFunctionType.Copy
ADD = mybir.AluOpType.add

P = 128
PACK = 4
LANES = 16
W2_SPLIT = 256
PIECES = ((0, 256), (256, 128), (384, 128))


def tile_picked_shuf3_relu_p_kernel(
    tc, x_words, x_scales, w1, w2, res, w3, offs, s1, s2, out
):
    nc = tc.nc
    with ExitStack() as ctx:
        lists = ctx.enter_context(tc.tile_pool(name="lists", bufs=1))
        sb = ctx.enter_context(tc.tile_pool(name="sb", bufs=1))
        psum = ctx.enter_context(tc.psum_pool(name="psum", bufs=1))

        def entries(list_tile, first, count):
            return list_tile[:, first // LANES : (first + count) // LANES]

        def mx(acc, codes_l, scales_l, codes_r, scales_r):
            nc.tensor.matmul_mx(
                out=acc,
                lhsT=codes_l.bitcast(FP8X4),
                lhsT_scale=scales_l,
                rhs=codes_r.bitcast(FP8X4),
                rhs_scale=scales_r,
                start=True,
                stop=True,
            )

        def quantize(codes, scales, grouped):
            nc.vector.quantize_mx(out=codes.bitcast(FP8X4), scales=scales, in_=grouped)

        offs_t = lists.tile([P, S // LANES], U16, name="offs_t")
        s1_t = lists.tile([P, S // LANES], U16, name="s1_t")
        s2_t = lists.tile([P, S // LANES], U16, name="s2_t")
        xw = sb.tile([P, T], U32, name="xw", align_bytes=64)
        xs = sb.tile([P, T], U8, name="xs", align_bytes=64)
        w1_raw = sb.tile([P, PACK, H], F32, name="w1_raw")
        w2_lo = sb.tile([P, PACK, 256], F32, name="w2_lo", align_bytes=64)
        reused = sb.tile([P, 512 + 1024], F32, name="reused", align_bytes=64)
        w2_raw = [w2_lo[:], reused[:, 512:1536].rearrange("p (j n) -> p j n", j=PACK)]
        w3_raw = sb.tile([P, PACK, N], F32, name="w3_raw", align_bytes=64)
        res_t = sb.tile([P, N // P, S], F32, name="res_t")

        nc.vector.memset(xs[:].bitcast(I32), 0)
        warm = sb.tile([P, 2], F32, name="warm")
        nc.gpsimd.memset(warm[:, 0:1], 0.0)
        nc.scalar.activation(warm[:, 1:2], warm[:, 0:1], RELU)
        w1_rows = w1.rearrange("(p j) n -> p j n", j=PACK)
        nc.sync.dma_start(w1_raw[:, 0, 0:256], w1_rows[:, 0, 0:256])
        nc.sync.dma_start(offs_t[:], offs)
        nc.sync.dma_start(s1_t[:], s1)
        nc.sync.dma_start(w1_raw[:, 0, 256:512], w1_rows[:, 0, 256:512])
        for j in range(1, PACK):
            nc.sync.dma_start(w1_raw[:, j, :], w1_rows[:, j, :])
        for q in range(4):
            nc.sync.dma_start(
                xs[32 * q : 32 * q + 4, :].bitcast(I32), x_scales[0, 4 * q : 4 * q + 4, :].bitcast(I32)
            )
        nc.sync.dma_start(xw[:].bitcast(I32), x_words[0].rearrange("p n t -> p (n t)").bitcast(I32))
        w2_rows = w2.rearrange("(p j) n -> p j n", j=PACK)
        nc.sync.dma_start(w2_raw[0], w2_rows[:, :, 0:W2_SPLIT])
        nc.sync.dma_start(w2_raw[1], w2_rows[:, :, W2_SPLIT:H])
        nc.sync.dma_start(w3_raw[:], w3.rearrange("(p j) n -> p j n", j=PACK))
        nc.sync.dma_start(s2_t[:], s2)
        nc.sync.dma_start(res_t[:], res.rearrange("(b p) j -> p b j", p=P))

        w1_codes = sb.tile([P, H], U32, name="w1_codes", align_bytes=64)
        w1_scales = sb.tile([P, H], U8, name="w1_scales", align_bytes=64)
        w1_dealt = w1_raw[:].rearrange("p j (m t) -> p m j t", t=PACK)
        w1_g = [sb.tile([P, 2, P, PACK], BF16, name="w1_g%d" % a, align_bytes=64) for a in range(2)]
        w1_out = [g[:].rearrange("p t m j -> p m j t") for g in w1_g]
        nc.vector.tensor_copy(w1_out[0], w1_dealt[:, :, :, 0:2])
        nc.scalar.copy(w1_out[1], w1_dealt[:, :, :, 2:4])
        xg_s = sb.tile([P, S], U8, name="xg_s", align_bytes=64)
        nc.vector.tensor_copy(xg_s[:], xs[:].indirect(offs_t[:]))
        for a in range(2):
            cols = slice(a * 256, (a + 1) * 256)
            quantize(w1_codes[:, cols], w1_scales[:, cols], w1_g[a][:].rearrange("p t m j -> p (t m j)"))
        xg_w = sb.tile([P, S], U32, name="xg_w", align_bytes=64)
        for a in range(2):
            nc.vector.tensor_copy(xg_w[:, a * 256 : (a + 1) * 256], xw[:].indirect(entries(offs_t, a * 256, 256)))

        def hidden_layer(label, codes_w, scales_w, codes, scales, first_bank):
            result = [sb.tile([P, S], F32, name="%s%d" % (label, t), align_bytes=64) for t in range(PACK)]
            bank = first_bank
            for t in range(PACK):
                rows = slice(t * P, (t + 1) * P)
                width = 256 if t == 0 else S
                for start in range(0, S, width):
                    cols = slice(start, start + width)
                    acc = psum.tile([P, width], F32, name="%s_acc%d" % (label, bank), tag="bank%d" % (bank % 8))
                    mx(acc[:], codes_w[:, rows], scales_w[:, rows], codes[:, cols], scales[:, cols])
                    nc.scalar.activation(result[t][:, cols], acc[:], RELU)
                    bank = bank + 1
            return result

        y = hidden_layer("y", w1_codes, w1_scales, xg_w, xg_s, 0)

        w2_g = sb.tile([P, PACK, P, PACK], BF16, name="w2_g", align_bytes=64)
        w2_out = w2_g[:].rearrange("p (u t) m j -> p u m j t", u=2)
        deal = "p j (m u t) -> p u m j t"
        nc.vector.tensor_copy(w2_out[:, :, 0 : W2_SPLIT // PACK], w2_raw[0].rearrange(deal, u=2, t=2))
        nc.scalar.copy(w2_out[:, :, W2_SPLIT // PACK : P], w2_raw[1].rearrange(deal, u=2, t=2))
        w2_codes = sb.tile([P, H], U32, name="w2_codes", align_bytes=64)
        w2_scales = sb.tile([P, H], U8, name="w2_scales", align_bytes=64)

        def gather(plane, rows_f32, list_tile, piece):
            first, count = piece
            for t in range(PACK):
                nc.vector.tensor_copy(
                    plane[:, t * count : (t + 1) * count], rows_f32[t][:].indirect(entries(list_tile, first, count))
                )

        def weave(woven, plane):
            nc.scalar.copy(
                woven.rearrange("p (c i t) -> p c t i", i=4, t=PACK),
                plane.rearrange("p (t c i) -> p c t i", i=4, t=PACK),
            )

        def pack(label, q, woven, tag):
            count = PIECES[q][1]
            codes = sb.tile([P, count], U32, name="%s_c%d" % (label, q), align_bytes=64, tag=tag)
            scales = sb.tile([P, count], U8, name="%s_s%d" % (label, q), align_bytes=64)
            quantize(codes[:], scales[:], woven)
            return codes, scales

        def stage(name, q, dtype, tag=""):
            return sb.tile([P, PACK * PIECES[q][1]], dtype, name=name, align_bytes=64, tag=tag or name)[:]

        z_woven = [sb.tile([P, 1024], BF16, name="z_w%d" % a, align_bytes=64) for a in range(2)]
        z_plane = [stage("z_p0", 0, F32), reused[:, 0:1024]]
        for a in range(2):
            gather(z_plane[a], y, s1_t, (256 * a, 256))
            weave(z_woven[a][:], z_plane[a])
        quantize(w2_codes[:], w2_scales[:], w2_g[:].rearrange("p t m j -> p (t m j)"))
        z_codes = sb.tile([P, S], U32, name="z_codes", align_bytes=64)
        z_scales = sb.tile([P, S], U8, name="z_scales", align_bytes=64)
        for a in range(2):
            quantize(z_codes[:, 256 * a : 256 * (a + 1)], z_scales[:, 256 * a : 256 * (a + 1)], z_woven[a][:])

        h = hidden_layer("h", w2_codes, w2_scales, z_codes, z_scales, 5)

        w3_src = w3_raw[:].rearrange("p j (c i) -> p c j i", i=4)
        w3_codes = [sb.tile([P, 256], U32, name="w3_codes%d" % a, align_bytes=64) for a in range(2)]
        w3_scales = [sb.tile([P, 256], U8, name="w3_scales%d" % a, align_bytes=64) for a in range(2)]
        for a, tag in enumerate(("reused", "z_scales")):
            w3_g = sb.tile([P, 256 * PACK], BF16, name="w3_g%d" % a, align_bytes=64, tag=tag)
            nc.scalar.copy(w3_g[:].rearrange("p (c i j) -> p c j i", i=4, j=PACK), w3_src[:, 64 * a : 64 * (a + 1)])
            quantize(w3_codes[a][:], w3_scales[a][:], w3_g[:])

        shared = sb.tile([P, 256 + 512], F32, name="shared", align_bytes=64, tag="w3_raw")
        zz_woven = [shared[:, 256:768].bitcast(BF16), stage("zz_w1", 1, BF16), stage("zz_w2", 2, BF16)]
        zz_plane = [stage("zz_p0", 0, F32), stage("zz_p1", 1, F32), shared[:, 0:512]]
        for q in range(2):
            gather(zz_plane[q], h, s2_t, PIECES[q])
            weave(zz_woven[q], zz_plane[q])
        z2 = [pack("zz", 0, zz_woven[0], "zz_c0")]
        gather(zz_plane[2], h, s2_t, PIECES[2])
        weave(zz_woven[2], zz_plane[2])
        z2.append(pack("zz", 1, zz_woven[1], "h3"))
        z2.append(pack("zz", 2, zz_woven[2], "zz_c2"))

        out_rows = out.rearrange("(b p) j -> p b j", p=P)
        bank = 0
        for (first, count), (codes, scales) in zip(PIECES, z2):
            per_bank = 2 if first + count == S else S // count
            for b0 in range(0, N // P, per_bank):
                acc = psum.tile([P, per_bank, count], F32, name="o_acc%d" % bank, tag="bank%d" % ((bank + 2) % 8))
                for b in range(per_bank):
                    half, rows = (b0 + b) // 2, slice((b0 + b) % 2 * P, ((b0 + b) % 2 + 1) * P)
                    mx(acc[:, b, :], w3_codes[half][:, rows], w3_scales[half][:, rows], codes[:], scales[:])
                o = sb.tile([P, per_bank, count], F32, name="o%d" % bank)
                nc.vector.tensor_tensor(o[:], acc[:], res_t[:, b0 : b0 + per_bank, first : first + count], ADD)
                nc.sync.dma_start(out_rows[:, b0 : b0 + per_bank, first : first + count], o[:])
                bank = bank + 1
